import numpy as np
import ml_dtypes


def mxq(x, axis, fmt="e4m3"):
    dtype, down = {"e4m3": (ml_dtypes.float8_e4m3fn, 7), "e5m2": (ml_dtypes.float8_e5m2, 14)}[fmt]
    v = np.moveaxis(np.asarray(x, np.float32).astype(ml_dtypes.bfloat16).astype(np.float64), axis, -1)
    blocks = v.reshape(v.shape[:-1] + (-1, 32))
    amax = np.abs(blocks).max(-1, keepdims=True)
    byte = np.maximum(np.where(amax > 0, np.frexp(amax)[1] - 1 + 127, 0) - down, 1)
    scale = np.exp2(byte - 127.0)
    codes = (blocks / scale).astype(np.float32).astype(dtype).astype(np.float64)
    return np.moveaxis((codes * scale).reshape(v.shape), -1, axis)


WIDE = False


def mx_kscale(k):
    if not WIDE:
        return np.ones(k)
    levels = np.array([10, -10, 5, -5, 0])
    if k % 512:
        return np.exp2(np.random.permutation(np.resize(levels, k // 32))).repeat(32)
    a = np.empty((k // 512, 16))
    for p in range(k // 512):
        a[p, :8] = np.random.permutation(np.resize(levels, 8))
        for g in range(8):
            far = levels[np.abs(levels - a[p, g]) >= 10]
            a[p, g + 8] = far[np.random.randint(len(far))]
    return np.exp2(a.ravel()).repeat(32)


def f64(x):
    return np.asarray(x).astype(np.float64)


def striped(idx):
    return np.tile(np.asarray(idx).reshape(-1, 16).T, (8, 1)).astype(np.uint16)


def unstriped(offs):
    return offs[:16].T.reshape(-1).astype(np.int64)


E2M1 = np.array([0.0, 0.5, 1.0, 1.5, 2.0, 3.0, 4.0, 6.0, -0.0, -0.5, -1.0, -1.5, -2.0, -3.0, -4.0, -6.0])


def pack_weight(w, fmt):
    k, n = w.shape
    w = f64(np.asarray(w, np.float32).astype(ml_dtypes.bfloat16)).reshape(k // 32, 32, n)
    amax = np.abs(w).max(1)
    if fmt == "e4m3":
        byte = np.frexp(amax)[1] - 1 + 127 - 7
    else:
        mant, ex = np.frexp(amax / 6.0)
        byte = np.where(mant > 0.5, ex, ex - 1) + 127
    byte = np.clip(np.where(amax > 0, byte, 1), 1, 254)
    scaled = (w * np.exp2(127.0 - byte)[:, None, :]).reshape(k, n).astype(np.float32)
    by_word = np.ascontiguousarray(scaled.reshape(k // 512, 128, 4, n).transpose(0, 1, 3, 2))
    if fmt == "e4m3":
        words = by_word.astype(ml_dtypes.float8_e4m3fn).view(np.uint8)
    else:
        c = by_word.astype(ml_dtypes.float4_e2m1fn).view(np.uint8) & 0xF
        words = (c[..., 0::2] | (c[..., 1::2] << 4)).reshape(k // 512, 128, 2 * n)
    return np.ascontiguousarray(words), np.ascontiguousarray(byte.astype(np.uint8).reshape(k // 512, 16, n))


def unpack_weight(words, scales, fmt):
    g, _, n = scales.shape
    words = np.ascontiguousarray(words).reshape(g, 128, n, -1)
    if fmt == "e4m3":
        vals = words.view(ml_dtypes.float8_e4m3fn).astype(np.float64)
    else:
        nib = np.empty((g, 128, n, 4), np.uint8)
        nib[..., 0::2] = words & 0xF
        nib[..., 1::2] = words >> 4
        vals = E2M1[nib]
    vals = vals * np.repeat(np.exp2(scales.astype(np.float64) - 127.0), 8, axis=1)[..., None]
    return vals.transpose(0, 1, 3, 2).reshape(g * 512, n)


def softplus(v):
    return np.log(1.0 + np.exp(v))


def sigmoid(v):
    return 1.0 / (1.0 + np.exp(-v))


D, E, T, I, Q = 512, 512, 2048, 512, 128


def setup_inputs():
    n = np.random.standard_normal
    idx = np.random.permutation(T)[:I]
    fd = mx_kscale(D)
    fe = mx_kscale(E)
    keysp = pack_weight(n((D, T)) / fd[:, None], "e2m1")
    valsp = pack_weight(n((E, T)) / fe[:, None], "e2m1")
    return {
        "query": (n((D, Q)) * 1.0 / np.sqrt(D) * fd[:, None]).astype(np.float32),
        "keys_words": keysp[0],
        "keys_scales": keysp[1],
        "ceil_t": np.tile(np.random.uniform(1.0, 4.0, T), (128, 1)).astype(np.float32),
        "halfp": np.tile(np.random.uniform(0.4, 1.5, T), (128, 1)).astype(np.float32),
        "wear": (np.random.uniform(0.0, 3.0, (Q, T))).astype(np.float32),
        "weary": (np.random.uniform(0.4, 1.5, (Q, 1))).astype(np.float32),
        "gout": (n((E, Q)) * 1 / np.sqrt(E) * fe[:, None]).astype(np.float32),
        "vals_words": valsp[0],
        "vals_scales": valsp[1],
        "dquery": (n((D, Q)) * 1.0 / np.sqrt(D) * fd[:, None]).astype(np.float32),
        "base": (0.5 * n((Q, T))).astype(np.float32),
        "offs": striped(idx),
    }


def reference(query, keys_words, keys_scales, ceil_t, halfp, wear, weary, gout, vals_words, vals_scales, dquery, base, offs):
    idx = unstriped(offs)
    keysu = unpack_weight(keys_words, keys_scales, "e2m1")
    valsu = unpack_weight(vals_words, vals_scales, "e2m1")
    queryq = mxq(f64(query), 0, "e4m3")
    keysidxg = keysu[:, idx]
    a = queryq.T @ keysidxg
    dqueryq = mxq(f64(dquery), 0, "e4m3")
    ta = dqueryq.T @ keysidxg
    fa = softplus(a * 2.0)
    s = fa * f64(ceil_t)[:1][:, idx] / (fa + f64(halfp)[:1][:, idx])
    p = np.exp(s) / (f64(wear)[:, idx] * f64(weary) + 1.0)
    goutq = mxq(f64(gout), 0, "e4m3")
    valsidxg = valsu[:, idx]
    c0 = goutq.T @ valsidxg
    dp = c0 / np.sum(p, axis=1, keepdims=True) + np.sum(c0 * p / np.square(np.sum(p, axis=1, keepdims=True)) * (-1.0), axis=1, keepdims=True)
    ds = dp / (f64(wear)[:, idx] * f64(weary) + 1.0) * np.exp(s)
    dfa = ds / (fa + f64(halfp)[:1][:, idx]) * f64(ceil_t)[:1][:, idx] - ds * fa * f64(ceil_t)[:1][:, idx] / np.square(fa + f64(halfp)[:1][:, idx])
    tfa = ta * 2.0 * sigmoid(a * 2.0)
    ts = (tfa * f64(ceil_t)[:1][:, idx] - tfa * fa * f64(ceil_t)[:1][:, idx] / (fa + f64(halfp)[:1][:, idx])) / (fa + f64(halfp)[:1][:, idx])
    tp = ts * np.exp(s) / (f64(wear)[:, idx] * f64(weary) + 1.0)
    tdp = np.sum(tp, axis=1, keepdims=True) * c0 / np.square(np.sum(p, axis=1, keepdims=True)) * (-1.0) + np.sum((tp * c0 - np.sum(tp, axis=1, keepdims=True) * np.sum(p, axis=1, keepdims=True) * 2.0 * c0 * p / np.square(np.sum(p, axis=1, keepdims=True))) / np.square(np.sum(p, axis=1, keepdims=True)) * (-1.0), axis=1, keepdims=True)
    tds = tdp / (f64(wear)[:, idx] * f64(weary) + 1.0) * np.exp(s) + ts * np.exp(s) * dp / (f64(wear)[:, idx] * f64(weary) + 1.0)
    tdfa = (tds - tfa * ds / (fa + f64(halfp)[:1][:, idx])) / (fa + f64(halfp)[:1][:, idx]) * f64(ceil_t)[:1][:, idx] - (tds * fa * f64(ceil_t)[:1][:, idx] + tfa * f64(ceil_t)[:1][:, idx] * ds - tfa * (fa + f64(halfp)[:1][:, idx]) * 2.0 * ds * fa * f64(ceil_t)[:1][:, idx] / np.square(fa + f64(halfp)[:1][:, idx])) / np.square(fa + f64(halfp)[:1][:, idx])
    tda = (tdfa * sigmoid(a * 2.0) + ta * 2.0 * sigmoid(a * 2.0) * (1.0 - sigmoid(a * 2.0)) * dfa) * 2.0
    gs = tda * 512.0
    gf = np.zeros((Q, T))
    gf[:, idx] = gs
    y = f64(base) + gf
    return y

from contextlib import ExitStack
import math

import concourse.mybir as mybir
from concourse.masks import make_identity

D, E, T, I, Q = 512, 512, 2048, 512, 128
P = 128
PACK = 4
FLOPS = 3 * 2 * D * Q * I
BYTES = 3 * D * Q * 4 + 2 * (P * 2 * T + 16 * T) + 2 * T * 4 + 3 * Q * T * 4 + Q * 4 + P * (I // 16) * 2

F32 = mybir.dt.float32
BF16 = mybir.dt.bfloat16
I32 = mybir.dt.int32
U32 = mybir.dt.uint32
U16 = mybir.dt.uint16
U8 = mybir.dt.uint8
FP8X4 = mybir.dt.float8_e4m3fn_x4
FP4X4 = mybir.dt.float4_e2m1fn_x4
ALU = mybir.AluOpType
ACT = mybir.ActivationFunctionType
AX = mybir.AxisListType
OUT_CHUNK = 512


def tile_attend_hvsaturating_wornout_s_kernel(tc, query, keys_words, keys_scales, ceil_t, halfp, wear, weary, gout,
                                               vals_words, vals_scales, dquery, base, offs, out):
    nc = tc.nc
    with ExitStack() as ctx:
        sb = ctx.enter_context(tc.tile_pool(name="sb", bufs=1))
        ps = ctx.enter_context(tc.psum_pool(name="ps", bufs=1))

        def slots(name):
            return sb.tile([P, I], F32, name=name)

        def column(name):
            return sb.tile([P, 1], F32, name=name)

        def bank(name):
            return ps.tile([P, I], F32, name=name)

        offsets = sb.tile([P, I // 16], U16, name="offsets")
        key_bytes = sb.tile([P, T], U8, name="key_bytes")
        val_bytes = sb.tile([P, T], U8, name="val_bytes")
        key_words = sb.tile([P, T], U16, name="key_words")
        val_words = sb.tile([P, T], U16, name="val_words")
        half_win = sb.tile([P, T], F32, name="half_win")
        ceil_win = sb.tile([P, T], F32, name="ceil_win")
        wear_win = sb.tile([P, T], F32, name="wear_win")
        weary_col = column("weary_col")

        nc.vector.memset(key_bytes[:].bitcast(I32), 0)
        nc.vector.memset(half_win[:].bitcast(I32), 0)
        nc.vector.memset(ceil_win[:].bitcast(I32), 0)
        nc.vector.memset(val_bytes[:].bitcast(I32), 0)

        def load_scale_rows(window, scales):
            for quad in range(4):
                nc.sync.dma_start(out=window[32 * quad:32 * quad + 4, :].bitcast(I32),
                                  in_=scales[0, 4 * quad:4 * quad + 4, :].bitcast(I32))

        def load_rows(name, src):
            raw = sb.tile([P, PACK, Q], F32, name=name)
            nc.sync.dma_start(out=raw[:], in_=src.rearrange("(p j) q -> p j q", j=PACK))
            return raw

        nc.sync.dma_start(offsets[:], offs)
        load_scale_rows(key_bytes, keys_scales)
        nc.sync.dma_start(out=key_words[:].bitcast(I32), in_=keys_words[0].bitcast(I32))
        query_raw = load_rows("query_raw", query)
        nc.scalar.dma_start(out=half_win[0:1, :], in_=halfp[0:1, :])
        nc.scalar.dma_start(out=ceil_win[0:1, :], in_=ceil_t[0:1, :])
        nc.sync.dma_start(out=weary_col[:], in_=weary)
        nc.sync.dma_start(out=wear_win[:], in_=wear)
        load_scale_rows(val_bytes, vals_scales)
        nc.sync.dma_start(out=val_words[:].bitcast(I32), in_=vals_words[0].bitcast(I32))
        dquery_raw = load_rows("dquery_raw", dquery)
        gout_raw = load_rows("gout_raw", gout)
        base_sb = sb.tile([P, T], F32, name="base_sb")
        nc.sync.dma_start(out=base_sb[:], in_=base)

        identity = sb.tile([P, P], F32, name="identity")
        make_identity(nc, identity[:])

        def quantise(name, raw):
            grouped = sb.tile([P, Q, PACK], BF16, name=name + "_grouped", tag=name + "_grouped", align_bytes=64)
            nc.gpsimd.tensor_scalar(grouped[:], raw[:].rearrange("p j q -> p q j"), 1.0, 0.0, ALU.mult, ALU.add)
            codes = sb.tile([P, Q], U32, name=name + "_codes", align_bytes=64)
            scales = sb.tile([P, Q], U8, name=name + "_scales", align_bytes=64)
            nc.vector.quantize_mx(out=codes[:].bitcast(FP8X4), scales=scales[:],
                                  in_=grouped[:].rearrange("p q j -> p (q j)"))
            return codes, scales

        def gather_packed(name, words, scale_bytes):
            listed_bytes = sb.tile([P, I], U8, name=name + "_listed_bytes", align_bytes=64)
            nc.vector.tensor_copy(listed_bytes[:], scale_bytes[:].indirect(offsets[:]))
            listed_words = sb.tile([P, I], U16, name=name + "_listed_words", align_bytes=64)
            nc.vector.tensor_copy(listed_words[:], words[:].indirect(offsets[:]))
            return listed_words, listed_bytes

        def product(name, rows, listed):
            acc = bank(name)
            nc.tensor.matmul_mx(out=acc[:], lhsT=rows[0][:].bitcast(FP8X4), lhsT_scale=rows[1][:],
                                rhs=listed[0][:].bitcast(FP4X4), rhs_scale=listed[1][:], start=True, stop=True)
            return acc

        keys_listed = gather_packed("keys", key_words, key_bytes)
        a = product("a", quantise("query", query_raw), keys_listed)

        def listed_down_partitions(name, window):
            row = slots(name + "_row")
            nc.scalar.activation(row[:], window[:].indirect(offsets[:]), ACT.Copy)
            turned = ps.tile([P, I // P, P], F32, name=name + "_turned")
            for j in range(I // P):
                nc.tensor.transpose(turned[:, j, :], row[:, j * P:(j + 1) * P], identity[:])
            return turned[:, :, 0]

        def spread(name, cols):
            wide = bank(name)
            for j in range(I // P):
                nc.tensor.transpose(wide[:, j * P:(j + 1) * P], cols[:, j:j + 1].to_broadcast([P, P]), identity[:])
            return wide

        half_turned = listed_down_partitions("half", half_win)
        ceil_turned = listed_down_partitions("ceil", ceil_win)
        shift_cols = sb.tile([P, I // P], F32, name="shift_cols")
        nc.vector.tensor_scalar(shift_cols[:], half_turned, 0.5, 0.5 * math.log(2.0), ALU.mult, ALU.add)
        shift = spread("shift", shift_cols)
        ceil_cols = sb.tile([P, I // P], F32, name="ceil_cols")
        nc.vector.tensor_copy(ceil_cols[:], ceil_turned)
        ch_cols = sb.tile([P, I // P], F32, name="ch_cols")
        nc.vector.tensor_tensor(ch_cols[:], half_turned, ceil_cols[:], ALU.mult)
        ceiling = spread("ceiling", ceil_cols)
        ch = spread("ch", ch_cols)

        th = slots("th")
        nc.scalar.activation(th[:], a[:], ACT.Tanh)
        abs_th = slots("abs_th")
        nc.vector.scalar_tensor_tensor(abs_th[:], th[:], -1.0, th[:], ALU.mult, ALU.max)

        weary_wide = slots("weary_wide")
        nc.gpsimd.tensor_scalar(weary_wide[:], weary_col[:].to_broadcast([P, I]), 1.0, 0.0, ALU.mult, ALU.add)
        worn = slots("worn")
        nc.vector.tensor_tensor(worn[:], wear_win[:].indirect(offsets[:]), weary_wide[:], ALU.mult)

        log_th = slots("log_th")
        nc.scalar.activation(log_th[:], abs_th[:], ACT.Ln, bias=1.0)
        rest = slots("rest")
        nc.vector.scalar_tensor_tensor(rest[:], log_th[:], -0.5, shift[:], ALU.mult, ALU.add)
        half_d = slots("half_d")
        nc.vector.scalar_tensor_tensor(half_d[:], a[:], 0.0, rest[:], ALU.max, ALU.add)

        den_sq = slots("den_sq")
        nc.scalar.activation(den_sq[:], worn[:], ACT.Square, bias=1.0)
        log_den_sq = slots("log_den_sq")
        nc.scalar.activation(log_den_sq[:], den_sq[:], ACT.Ln)
        d_sq = slots("d_sq")
        nc.scalar.activation(d_sq[:], half_d[:], ACT.Square, scale=2.0)
        log_d_sq = slots("log_d_sq")
        nc.scalar.activation(log_d_sq[:], d_sq[:], ACT.Ln)
        inv_d_sq = slots("inv_d_sq")
        nc.scalar.activation(inv_d_sq[:], log_d_sq[:], ACT.Exp, scale=-1.0)

        ch_d = slots("ch_d")
        nc.vector.scalar_tensor_tensor(ch_d[:], half_d[:], 2.0, ch[:], ALU.mult, ALU.mult)
        top = slots("top")
        nc.vector.tensor_tensor(top[:], ceiling[:], log_den_sq[:], ALU.subtract)
        ta = product("ta", quantise("dquery", dquery_raw), keys_listed)
        vals_listed = gather_packed("vals", val_words, val_bytes)
        c0 = product("c0", quantise("gout", gout_raw), vals_listed)
        placed = sb.tile([P, T], F32, name="placed", tag="gout_grouped", align_bytes=64)
        nc.gpsimd.memset(placed[:], 0.0)
        bend0 = slots("bend0")
        nc.vector.scalar_tensor_tensor(bend0[:], half_d[:], -4.0, ch[:], ALU.mult, ALU.add)
        bend = slots("bend")
        nc.vector.tensor_tensor(bend[:], bend0[:], d_sq[:], ALU.subtract)

        drop = slots("drop")
        nc.vector.tensor_tensor(drop[:], ch_d[:], inv_d_sq[:], ALU.mult)
        score = slots("score")
        nc.vector.tensor_tensor(score[:], top[:], drop[:], ALU.subtract)
        neg_max = column("neg_max")
        nc.vector.tensor_reduce(neg_max[:], score[:], AX.X, ALU.max, negate=True)
        lifted = slots("lifted")
        nc.scalar.activation(lifted[:], score[:], ACT.Exp, bias=neg_max[:])
        u_inv = slots("u_inv")
        nc.vector.scalar_tensor_tensor(u_inv[:], th[:], 1.0, inv_d_sq[:], ALU.add, ALU.mult)
        part = slots("part")
        total = column("total")
        nc.vector.scalar_tensor_tensor(part[:], worn[:], 1.0, lifted[:], ALU.add, ALU.mult, accum_out=total[:])
        slope = slots("slope")
        nc.vector.scalar_tensor_tensor(slope[:], u_inv[:], -512.0, ch[:], ALU.mult, ALU.mult)
        inv_total = column("inv_total")
        nc.vector.reciprocal(inv_total[:], total[:])
        curve = slots("curve")
        nc.vector.tensor_tensor(curve[:], u_inv[:], bend[:], ALU.mult)
        weighted_c0 = slots("weighted_c0")
        mean_c0 = column("mean_c0")
        nc.vector.scalar_tensor_tensor(weighted_c0[:], c0[:], inv_total[:], part[:], ALU.mult, ALU.mult,
                                       accum_out=mean_c0[:])
        below = slots("below")
        nc.scalar.activation(below[:], c0[:], ACT.Identity, bias=mean_c0[:], scale=-1.0)
        lead = slots("lead")
        nc.vector.scalar_tensor_tensor(lead[:], part[:], inv_total[:], slope[:], ALU.mult, ALU.mult)
        move = slots("move")
        nc.vector.scalar_tensor_tensor(move[:], curve[:], 2.0, ta[:], ALU.add, ALU.mult)
        weighted_ts = slots("weighted_ts")
        mean_ts = column("mean_ts")
        nc.vector.scalar_tensor_tensor(weighted_ts[:], lead[:], -1.0 / 512.0, ta[:], ALU.mult, ALU.mult,
                                       accum_out=mean_ts[:])
        cov_terms = slots("cov_terms")
        neg_cov = column("neg_cov")
        nc.vector.scalar_tensor_tensor(cov_terms[:], weighted_ts[:], 1.0, below[:], ALU.mult, ALU.mult,
                                       accum_out=neg_cov[:])
        inner0 = slots("inner0")
        nc.vector.scalar_tensor_tensor(inner0[:], move[:], mean_ts[:], below[:], ALU.subtract, ALU.mult)
        inner = slots("inner")
        nc.vector.tensor_scalar(inner[:], inner0[:], neg_cov[:], None, ALU.subtract)
        nc.vector.tensor_tensor(placed[:].indirect(offsets[:]), inner[:], lead[:], ALU.mult)

        for c in range(T // OUT_CHUNK):
            cols = slice(c * OUT_CHUNK, (c + 1) * OUT_CHUNK)
            result = sb.tile([P, OUT_CHUNK], F32, name="result%d" % c)
            nc.vector.tensor_tensor(result[:], placed[:, cols], base_sb[:, cols], ALU.add)
            nc.sync.dma_start(out=out[:, cols], in_=result[:])
